import numpy as np
import ml_dtypes

BF16 = ml_dtypes.bfloat16


def bf(x):
    return np.asarray(x, np.float32).astype(BF16)


def f32(x):
    return np.asarray(x, np.float32)


def f64(x):
    return np.asarray(x).astype(np.float64)


def striped(idx):
    return np.tile(idx.reshape(-1, 16).T, (8, 1))


def rows(idx, k):
    return np.tile(idx, (k, 1))


def look(tab, idx):
    return np.take_along_axis(f64(tab), rows(idx, len(tab)), axis=1)


K, S, V, N, M = 256, 256, 256, 256, 256


def setup_inputs():
    return {"tab": bf(0.5 * np.random.standard_normal((K, S))), "y": f32(np.random.standard_normal((K, V))), "w": bf(np.random.standard_normal((K, M)) / np.sqrt(K)), "offs": striped(np.random.permutation(S)[:N])}


def reference(tab, y, w, offs):
    idx = offs[:16].T.reshape(-1)
    t = look(tab, idx)
    x = np.exp(t) * f64(y)
    y = f64(w).T @ x
    return y

@@ -1,0 +1,60 @@
+import concourse.mybir as mybir
+
+P = 128
+ROWS = 256
+COLS = 256
+OUTS = 256
+PIECE = 128
+BLOCKS = ROWS // P
+PIECES = COLS // PIECE
+OUT_BLOCKS = OUTS // P
+
+BF16, F32, U16 = mybir.dt.bfloat16, mybir.dt.float32, mybir.dt.uint16
+EXP = mybir.ActivationFunctionType.Exp
+MULT = mybir.AluOpType.mult
+
+FLOPS = 2 * ROWS * OUTS * COLS
+
+
+def tile_lookup_gate_exp_none_kernel(tc, tab, y, w, offs, out):
+    nc = tc.nc
+    with (
+        tc.tile_pool(name="held", bufs=1) as held,
+        tc.tile_pool(name="work", bufs=2 * PIECES) as work,
+        tc.psum_pool(name="psum", bufs=PIECES) as psum,
+    ):
+        offsets = held.tile([P, COLS // 16], U16, name="offsets")
+        nc.sync.dma_start(offsets[:], offs)
+
+        tables = []
+        for k in range(BLOCKS):
+            table = held.tile([P, COLS], BF16, name=f"table{k}")
+            nc.sync.dma_start(table[:], tab.rearrange("(p k) s -> k p s", k=BLOCKS)[k])
+            tables.append(table)
+        stream = held.tile([P, BLOCKS, COLS], F32, name="stream")
+        nc.scalar.dma_start(stream[:], y.rearrange("(p k) j -> p k j", k=BLOCKS))
+        weights = held.tile([P, BLOCKS, OUTS], BF16, name="weights")
+        nc.sync.dma_start(weights[:], w.rearrange("(p k) m -> p k m", k=BLOCKS))
+
+        out_rows = out.rearrange("(m p) j -> m p j", p=P)
+        for piece in range(PIECES):
+            columns = slice(piece * PIECE, (piece + 1) * PIECE)
+            picks = offsets[:, piece * PIECE // 16 : (piece + 1) * PIECE // 16]
+            sums = [psum.tile([P, PIECE], F32, name=f"sums{m}") for m in range(OUT_BLOCKS)]
+            for k in range(BLOCKS):
+                gate = work.tile([P, PIECE], F32, name="gate")
+                nc.scalar.activation(gate[:], tables[k][:].indirect(picks), EXP)
+                x = work.tile([P, PIECE], BF16, name="x")
+                nc.vector.tensor_tensor(x[:], gate[:], stream[:, k, columns], MULT)
+                for m in range(OUT_BLOCKS):
+                    nc.tensor.matmul(
+                        sums[m][:],
+                        weights[:, k, m * P : (m + 1) * P],
+                        x[:],
+                        start=(k == 0),
+                        stop=(k == BLOCKS - 1),
+                    )
+            for m in range(OUT_BLOCKS):
+                result = work.tile([P, PIECE], F32, name="result")
+                nc.vector.tensor_copy(result[:], sums[m][:])
+                nc.sync.dma_start(out_rows[m][:, columns], result[:])

@@ -23,6 +23,11 @@ def tile_lookup_gate_exp_none_kernel(tc, tab, y, w, offs, out):
         tc.tile_pool(name="work", bufs=2 * PIECES) as work,
         tc.psum_pool(name="psum", bufs=PIECES) as psum,
     ):
+        warm_in = held.tile([P, 1], F32, name="warm_in")
+        nc.vector.memset(warm_in[:], 0.0)
+        warm_out = held.tile([P, 1], F32, name="warm_out")
+        nc.scalar.activation(warm_out[:], warm_in[:], EXP)
+
         offsets = held.tile([P, COLS // 16], U16, name="offsets")
         nc.sync.dma_start(offsets[:], offs)
 

@@ -23,29 +23,30 @@ def tile_lookup_gate_exp_none_kernel(tc, tab, y, w, offs, out):
         tc.tile_pool(name="work", bufs=2 * PIECES) as work,
         tc.psum_pool(name="psum", bufs=PIECES) as psum,
     ):
-        warm_in = held.tile([P, 1], F32, name="warm_in")
-        nc.vector.memset(warm_in[:], 0.0)
-        warm_out = held.tile([P, 1], F32, name="warm_out")
-        nc.scalar.activation(warm_out[:], warm_in[:], EXP)
-
         offsets = held.tile([P, COLS // 16], U16, name="offsets")
         nc.sync.dma_start(offsets[:], offs)
 
-        tables = []
-        for k in range(BLOCKS):
-            table = held.tile([P, COLS], BF16, name=f"table{k}")
-            nc.sync.dma_start(table[:], tab.rearrange("(p k) s -> k p s", k=BLOCKS)[k])
-            tables.append(table)
+        tab_rows = tab.rearrange("(p k) s -> k p s", k=BLOCKS)
+        tables = [held.tile([P, COLS], BF16, name=f"table{k}") for k in range(BLOCKS)]
+        nc.scalar.dma_start(tables[0][:], tab_rows[0])
+        nc.sync.dma_start(tables[1][:], tab_rows[1])
         stream = held.tile([P, BLOCKS, COLS], F32, name="stream")
         nc.scalar.dma_start(stream[:], y.rearrange("(p k) j -> p k j", k=BLOCKS))
         weights = held.tile([P, BLOCKS, OUTS], BF16, name="weights")
         nc.sync.dma_start(weights[:], w.rearrange("(p k) m -> p k m", k=BLOCKS))
 
+        warm_in = held.tile([P, 1], F32, name="warm_in")
+        nc.vector.memset(warm_in[:], 0.0)
+        warm_out = held.tile([P, 1], F32, name="warm_out")
+        nc.scalar.activation(warm_out[:], warm_in[:], EXP)
+
         out_rows = out.rearrange("(m p) j -> m p j", p=P)
+        sums = {}
         for piece in range(PIECES):
             columns = slice(piece * PIECE, (piece + 1) * PIECE)
             picks = offsets[:, piece * PIECE // 16 : (piece + 1) * PIECE // 16]
-            sums = [psum.tile([P, PIECE], F32, name=f"sums{m}") for m in range(OUT_BLOCKS)]
+            for m in range(OUT_BLOCKS):
+                sums[piece, m] = psum.tile([P, PIECE], F32, name=f"sums{m}")
             for k in range(BLOCKS):
                 gate = work.tile([P, PIECE], F32, name="gate")
                 nc.scalar.activation(gate[:], tables[k][:].indirect(picks), EXP)
@@ -53,13 +54,18 @@ def tile_lookup_gate_exp_none_kernel(tc, tab, y, w, offs, out):
                 nc.vector.tensor_tensor(x[:], gate[:], stream[:, k, columns], MULT)
                 for m in range(OUT_BLOCKS):
                     nc.tensor.matmul(
-                        sums[m][:],
+                        sums[piece, m][:],
                         weights[:, k, m * P : (m + 1) * P],
                         x[:],
                         start=(k == 0),
                         stop=(k == BLOCKS - 1),
                     )
-            for m in range(OUT_BLOCKS):
-                result = work.tile([P, PIECE], F32, name="result")
-                nc.vector.tensor_copy(result[:], sums[m][:])
-                nc.sync.dma_start(out_rows[m][:, columns], result[:])
+
+        for piece in range(PIECES):
+            columns = slice(piece * PIECE, (piece + 1) * PIECE)
+            upper = work.tile([P, PIECE], F32, name="upper")
+            nc.vector.tensor_copy(upper[:], sums[piece, 0][:])
+            nc.sync.dma_start(out_rows[0][:, columns], upper[:])
+            lower = work.tile([P, PIECE], F32, name="lower")
+            nc.scalar.copy(lower[:], sums[piece, 1][:])
+            nc.scalar.dma_start(out_rows[1][:, columns], lower[:])

@@ -23,22 +23,22 @@ def tile_lookup_gate_exp_none_kernel(tc, tab, y, w, offs, out):
         tc.tile_pool(name="work", bufs=2 * PIECES) as work,
         tc.psum_pool(name="psum", bufs=PIECES) as psum,
     ):
+        warm_in = held.tile([P, 1], F32, name="warm_in")
+        nc.vector.memset(warm_in[:], 0.0)
+        warm_out = held.tile([P, 1], F32, name="warm_out")
+        nc.scalar.activation(warm_out[:], warm_in[:], EXP)
+
         offsets = held.tile([P, COLS // 16], U16, name="offsets")
         nc.sync.dma_start(offsets[:], offs)
 
         tab_rows = tab.rearrange("(p k) s -> k p s", k=BLOCKS)
         tables = [held.tile([P, COLS], BF16, name=f"table{k}") for k in range(BLOCKS)]
-        nc.scalar.dma_start(tables[0][:], tab_rows[0])
-        nc.sync.dma_start(tables[1][:], tab_rows[1])
+        for k in range(BLOCKS):
+            nc.sync.dma_start(tables[k][:], tab_rows[k])
         stream = held.tile([P, BLOCKS, COLS], F32, name="stream")
-        nc.scalar.dma_start(stream[:], y.rearrange("(p k) j -> p k j", k=BLOCKS))
+        nc.sync.dma_start(stream[:], y.rearrange("(p k) j -> p k j", k=BLOCKS))
         weights = held.tile([P, BLOCKS, OUTS], BF16, name="weights")
         nc.sync.dma_start(weights[:], w.rearrange("(p k) m -> p k m", k=BLOCKS))
-
-        warm_in = held.tile([P, 1], F32, name="warm_in")
-        nc.vector.memset(warm_in[:], 0.0)
-        warm_out = held.tile([P, 1], F32, name="warm_out")
-        nc.scalar.activation(warm_out[:], warm_in[:], EXP)
 
         out_rows = out.rearrange("(m p) j -> m p j", p=P)
         sums = {}

@@ -13,6 +13,9 @@ BF16, F32, U16 = mybir.dt.bfloat16, mybir.dt.float32, mybir.dt.uint16
 EXP = mybir.ActivationFunctionType.Exp
 MULT = mybir.AluOpType.mult
 
+WARM_COLS = 512
+WARM_MATMULS = 5
+
 FLOPS = 2 * ROWS * OUTS * COLS
 
 
@@ -27,6 +30,12 @@ def tile_lookup_gate_exp_none_kernel(tc, tab, y, w, offs, out):
         nc.vector.memset(warm_in[:], 0.0)
         warm_out = held.tile([P, 1], F32, name="warm_out")
         nc.scalar.activation(warm_out[:], warm_in[:], EXP)
+
+        zeros = held.tile([P, WARM_COLS], BF16, name="zeros")
+        nc.vector.memset(zeros[:], 0.0)
+        warm_sums = psum.tile([P, WARM_COLS], F32, name="warm_sums", bufs=1)
+        for i in range(WARM_MATMULS):
+            nc.tensor.matmul(warm_sums[:], zeros[:, :P], zeros[:], start=True, stop=True)
 
         offsets = held.tile([P, COLS // 16], U16, name="offsets")
         nc.sync.dma_start(offsets[:], offs)

import concourse.mybir as mybir

P = 128
ROWS = 256
COLS = 256
OUTS = 256
PIECE = 128
BLOCKS = ROWS // P
PIECES = COLS // PIECE
OUT_BLOCKS = OUTS // P

BF16, F32, U16 = mybir.dt.bfloat16, mybir.dt.float32, mybir.dt.uint16
EXP = mybir.ActivationFunctionType.Exp
MULT = mybir.AluOpType.mult

WARM_COLS = 512
WARM_MATMULS = 5

FLOPS = 2 * ROWS * OUTS * COLS


def tile_lookup_gate_exp_none_kernel(tc, tab, y, w, offs, out):
    nc = tc.nc
    with (
        tc.tile_pool(name="held", bufs=1) as held,
        tc.tile_pool(name="work", bufs=2 * PIECES) as work,
        tc.psum_pool(name="psum", bufs=PIECES) as psum,
    ):
        warm_in = held.tile([P, 1], F32, name="warm_in")
        nc.vector.memset(warm_in[:], 0.0)
        warm_out = held.tile([P, 1], F32, name="warm_out")
        nc.scalar.activation(warm_out[:], warm_in[:], EXP)

        zeros = held.tile([P, WARM_COLS], BF16, name="zeros")
        nc.vector.memset(zeros[:], 0.0)
        warm_sums = psum.tile([P, WARM_COLS], F32, name="warm_sums", bufs=1)
        for i in range(WARM_MATMULS):
            nc.tensor.matmul(warm_sums[:], zeros[:, :P], zeros[:], start=True, stop=True)

        offsets = held.tile([P, COLS // 16], U16, name="offsets")
        nc.sync.dma_start(offsets[:], offs)

        tab_rows = tab.rearrange("(p k) s -> k p s", k=BLOCKS)
        tables = [held.tile([P, COLS], BF16, name=f"table{k}") for k in range(BLOCKS)]
        for k in range(BLOCKS):
            nc.sync.dma_start(tables[k][:], tab_rows[k])
        stream = held.tile([P, BLOCKS, COLS], F32, name="stream")
        nc.sync.dma_start(stream[:], y.rearrange("(p k) j -> p k j", k=BLOCKS))
        weights = held.tile([P, BLOCKS, OUTS], BF16, name="weights")
        nc.sync.dma_start(weights[:], w.rearrange("(p k) m -> p k m", k=BLOCKS))

        out_rows = out.rearrange("(m p) j -> m p j", p=P)
        sums = {}
        for piece in range(PIECES):
            columns = slice(piece * PIECE, (piece + 1) * PIECE)
            picks = offsets[:, piece * PIECE // 16 : (piece + 1) * PIECE // 16]
            for m in range(OUT_BLOCKS):
                sums[piece, m] = psum.tile([P, PIECE], F32, name=f"sums{m}")
            for k in range(BLOCKS):
                gate = work.tile([P, PIECE], F32, name="gate")
                nc.scalar.activation(gate[:], tables[k][:].indirect(picks), EXP)
                x = work.tile([P, PIECE], BF16, name="x")
                nc.vector.tensor_tensor(x[:], gate[:], stream[:, k, columns], MULT)
                for m in range(OUT_BLOCKS):
                    nc.tensor.matmul(
                        sums[piece, m][:],
                        weights[:, k, m * P : (m + 1) * P],
                        x[:],
                        start=(k == 0),
                        stop=(k == BLOCKS - 1),
                    )

        for piece in range(PIECES):
            columns = slice(piece * PIECE, (piece + 1) * PIECE)
            upper = work.tile([P, PIECE], F32, name="upper")
            nc.vector.tensor_copy(upper[:], sums[piece, 0][:])
            nc.sync.dma_start(out_rows[0][:, columns], upper[:])
            lower = work.tile([P, PIECE], F32, name="lower")
            nc.scalar.copy(lower[:], sums[piece, 1][:])
            nc.scalar.dma_start(out_rows[1][:, columns], lower[:])
